import numpy as np
import ml_dtypes


def mxq(x, axis, fmt="e4m3"):
    dtype, down = {"e4m3": (ml_dtypes.float8_e4m3fn, 7), "e5m2": (ml_dtypes.float8_e5m2, 14)}[fmt]
    v = np.moveaxis(np.asarray(x, np.float32).astype(ml_dtypes.bfloat16).astype(np.float64), axis, -1)
    blocks = v.reshape(v.shape[:-1] + (-1, 32))
    amax = np.abs(blocks).max(-1, keepdims=True)
    byte = np.maximum(np.where(amax > 0, np.frexp(amax)[1] - 1 + 127, 0) - down, 1)
    scale = np.exp2(byte - 127.0)
    codes = (blocks / scale).astype(np.float32).astype(dtype).astype(np.float64)
    return np.moveaxis((codes * scale).reshape(v.shape), -1, axis)


WIDE = False


def mx_kscale(k):
    if not WIDE:
        return np.ones(k)
    levels = np.array([10, -10, 5, -5, 0])
    if k % 512:
        return np.exp2(np.random.permutation(np.resize(levels, k // 32))).repeat(32)
    a = np.empty((k // 512, 16))
    for p in range(k // 512):
        a[p, :8] = np.random.permutation(np.resize(levels, 8))
        for g in range(8):
            far = levels[np.abs(levels - a[p, g]) >= 10]
            a[p, g + 8] = far[np.random.randint(len(far))]
    return np.exp2(a.ravel()).repeat(32)


def f64(x):
    return np.asarray(x).astype(np.float64)


def striped8(idx):
    return np.concatenate([v.reshape(-1, 16).T for v in idx]).astype(np.uint16)


def unstriped8(offs):
    return np.stack([offs[16 * g:16 * g + 16].T.reshape(-1) for g in range(8)]).astype(np.int64)


E2M1 = np.array([0.0, 0.5, 1.0, 1.5, 2.0, 3.0, 4.0, 6.0, -0.0, -0.5, -1.0, -1.5, -2.0, -3.0, -4.0, -6.0])


def pack_weight(w, fmt):
    k, n = w.shape
    w = f64(np.asarray(w, np.float32).astype(ml_dtypes.bfloat16)).reshape(k // 32, 32, n)
    amax = np.abs(w).max(1)
    if fmt == "e4m3":
        byte = np.frexp(amax)[1] - 1 + 127 - 7
    else:
        mant, ex = np.frexp(amax / 6.0)
        byte = np.where(mant > 0.5, ex, ex - 1) + 127
    byte = np.clip(np.where(amax > 0, byte, 1), 1, 254)
    scaled = (w * np.exp2(127.0 - byte)[:, None, :]).reshape(k, n).astype(np.float32)
    by_word = np.ascontiguousarray(scaled.reshape(k // 512, 128, 4, n).transpose(0, 1, 3, 2))
    if fmt == "e4m3":
        words = by_word.astype(ml_dtypes.float8_e4m3fn).view(np.uint8)
    else:
        c = by_word.astype(ml_dtypes.float4_e2m1fn).view(np.uint8) & 0xF
        words = (c[..., 0::2] | (c[..., 1::2] << 4)).reshape(k // 512, 128, 2 * n)
    return np.ascontiguousarray(words), np.ascontiguousarray(byte.astype(np.uint8).reshape(k // 512, 16, n))


def unpack_weight(words, scales, fmt):
    g, _, n = scales.shape
    words = np.ascontiguousarray(words).reshape(g, 128, n, -1)
    if fmt == "e4m3":
        vals = words.view(ml_dtypes.float8_e4m3fn).astype(np.float64)
    else:
        nib = np.empty((g, 128, n, 4), np.uint8)
        nib[..., 0::2] = words & 0xF
        nib[..., 1::2] = words >> 4
        vals = E2M1[nib]
    vals = vals * np.repeat(np.exp2(scales.astype(np.float64) - 127.0), 8, axis=1)[..., None]
    return vals.transpose(0, 1, 3, 2).reshape(g * 512, n)


K, M, T, S = 1536, 512, 2048, 512


def setup_inputs():
    n = np.random.standard_normal
    s = mx_kscale(K)[:, None]
    p_w = pack_weight(n((K, M)) / np.sqrt(K) / s, "e4m3")
    return {
        "xT": (n((K, T)) * s).astype(np.float32),
        "w_words": p_w[0],
        "w_scales": p_w[1],
        "wgt": np.repeat(np.random.uniform(0.5, 2.0, (8, S)), 16, axis=0).astype(np.float32),
        "offs": striped8(np.stack([np.random.permutation(T)[:S] for _ in range(8)])),
    }


def reference(xT, w_words, w_scales, wgt, offs):
    idx = unstriped8(offs)
    group = np.arange(K) % 512 // 64
    xg = f64(wgt)[np.arange(K) // 4 % 128] * f64(xT)[np.arange(K)[:, None], idx[group]]
    xT_ = mxq(xg, 0, "e4m3")
    w_ = unpack_weight(w_words, w_scales, "e4m3")
    y = w_.T @ xT_
    return y

@@ -1,0 +1,151 @@
+from contextlib import ExitStack
+
+import concourse.mybir as mybir
+
+K, M, T, S = 1536, 512, 2048, 512
+FLOPS = 2 * K * M * S
+
+F32 = mybir.dt.float32
+BF16 = mybir.dt.bfloat16
+I32 = mybir.dt.int32
+U8 = mybir.dt.uint8
+U16 = mybir.dt.uint16
+U32 = mybir.dt.uint32
+FP8X4 = mybir.dt.float8_e4m3fn_x4
+MULT = mybir.AluOpType.mult
+
+P = 128
+PASSES = K // (4 * P)
+HALF = S // 2
+LIST_COLS = HALF // 16
+MT = M // P
+
+
+def tile_list_heads_none_kernel(tc, xT, w_words, w_scales, wgt, offs, out):
+    nc = tc.nc
+    with ExitStack() as ctx:
+        keep = ctx.enter_context(tc.tile_pool(name="keep", bufs=1))
+        psum = ctx.enter_context(tc.psum_pool(name="psum", bufs=1))
+
+        offsets = keep.tile([P, S // 16], U16, name="offsets")
+        wgt_sb = keep.tile([P, S], F32, name="wgt_sb", align_bytes=64)
+        wgt_rows = keep.tile([P, 32], F32, name="wgt_rows", align_bytes=64)
+        wgt_cols = keep.tile([P, 32], F32, name="wgt_cols", align_bytes=64)
+        wgt_spread = keep.tile([P, S], F32, name="wgt_spread", align_bytes=64)
+        nc.scalar.dma_start(wgt_rows[:], wgt.rearrange("(g r) (b q) -> g r b q", r=16, q=32)[:, 0, :, :])
+        nc.vector.transpose(wgt_cols[:], wgt_rows[:])
+        nc.vector.tensor_copy(
+            wgt_spread[:].rearrange("p (b e r) -> p b e r", e=2, r=16),
+            wgt_cols[:].rearrange("p (e b) -> p b e", e=2).unsqueeze(3).to_broadcast([P, S // 32, 2, 16]),
+        )
+        nc.vector.transpose(wgt_sb[:], wgt_spread[:])
+
+        w_planes = keep.tile([P, M], U8, name="w_planes", align_bytes=64)
+        nc.gpsimd.memset(w_planes[:].bitcast(I32), 0)
+        for q in range(4):
+            nc.gpsimd.dma_start(
+                w_planes[32 * q : 32 * q + 4 * PASSES, :].bitcast(I32),
+                w_scales[:, 4 * q : 4 * q + 4, :].bitcast(I32),
+            )
+
+        w_sb = [keep.tile([P, M], I32, name="w_sb%d" % a, align_bytes=256) for a in range(PASSES)]
+
+        def load_w(a):
+            nc.sync.dma_start(w_sb[a][:], w_words[a].rearrange("p n t -> p (n t)").bitcast(I32))
+
+        x_sb = {}
+        for a in range(PASSES):
+            rows = xT[4 * P * a : 4 * P * (a + 1), :].rearrange("(p t) c -> p t c", t=4)
+            for t in range(4):
+                x_sb[a, t] = keep.tile([P, T], F32, name="x%d%d" % (a, t), align_bytes=256)
+                if (a, t) == (2, 3):
+                    load_w(0)
+                nc.sync.dma_start(x_sb[a, t][:], rows[:, t, :])
+                if (a, t) == (0, 0):
+                    nc.sync.dma_start(offsets[:], offs)
+        load_w(1)
+        load_w(2)
+
+        g, xb, codes, scales = {}, {}, {}, {}
+        for a in range(PASSES):
+            for h in range(2):
+                g[a, h] = keep.tile([P, 4, HALF], F32, name="g%d%d" % (a, h))
+                xb[a, h] = keep.tile([P, HALF, 4], BF16, name="xb%d%d" % (a, h), align_bytes=64)
+                codes[a, h] = keep.tile([P, HALF], U32, name="codes%d%d" % (a, h), align_bytes=64)
+                scales[a, h] = keep.tile([P, HALF], U8, name="scales%d%d" % (a, h), align_bytes=64)
+        acc = {}
+        for h in range(2):
+            for m in range(MT):
+                acc[m, h] = psum.tile([P, HALF], F32, name="acc%d%d" % (m, h))
+
+        def gather(a, t, h, c0=0, c1=HALF):
+            j0, j1 = h * HALF + c0, h * HALF + c1
+            nc.vector.tensor_tensor(
+                g[a, h][:, t, c0:c1],
+                x_sb[a, t][:].indirect(offsets[:, j0 // 16 : j1 // 16]),
+                wgt_sb[:, j0:j1],
+                MULT,
+            )
+
+        def interleave(copy, a, h, t0, t1, c0=0, c1=HALF):
+            copy(xb[a, h][:, c0:c1, t0:t1], g[a, h][:, t0:t1, c0:c1].rearrange("p t n -> p n t"))
+
+        def quantize(a, h):
+            nc.vector.quantize_mx(
+                out=codes[a, h][:].bitcast(FP8X4),
+                scales=scales[a, h][:],
+                in_=xb[a, h][:].rearrange("p n t -> p (n t)"),
+            )
+
+        def multiply(a, h):
+            for m in range(MT):
+                cols = slice(m * P, (m + 1) * P)
+                nc.tensor.matmul_mx(
+                    out=acc[m, h][:],
+                    lhsT=w_sb[a][:, cols].bitcast(FP8X4),
+                    lhsT_scale=w_planes[4 * a : P, cols],
+                    rhs=codes[a, h][:].bitcast(FP8X4),
+                    rhs_scale=scales[a, h][:],
+                    start=(a == 0),
+                    stop=(a == PASSES - 1),
+                )
+
+        last = PASSES - 1
+        for a in range(PASSES):
+            for t in range(3 if a == last else 4):
+                for h in range(2):
+                    gather(a, t, h)
+                if t == 0 and a > 0:
+                    for h in range(2):
+                        quantize(a - 1, h)
+                        multiply(a - 1, h)
+                if a == last and t == 1:
+                    for h in range(2):
+                        interleave(nc.scalar.copy, a, h, 0, 2)
+            if a < last:
+                for h in range(2):
+                    interleave(nc.scalar.copy, a, h, 0, 4)
+
+        out_v = out.rearrange("(m p) j -> p m j", p=P)
+        res = [keep.tile([P, MT, HALF], F32, name="res%d" % h, align_bytes=256) for h in range(2)]
+        mid = HALF // 2
+        gather(last, 3, 0, 0, mid)
+        interleave(nc.scalar.copy, last, 0, 2, 4, 0, mid)
+        gather(last, 3, 0, mid, HALF)
+        gather(last, 3, 1, 0, mid)
+        interleave(nc.scalar.copy, last, 1, 2, 4, 0, mid)
+        interleave(nc.vector.tensor_copy, last, 0, 2, 4, mid, HALF)
+        quantize(last, 0)
+        multiply(last, 0)
+        gather(last, 3, 1, mid, HALF)
+        interleave(nc.vector.tensor_copy, last, 1, 2, 4, mid, HALF)
+        quantize(last, 1)
+        multiply(last, 1)
+        for h in range(2):
+            cols = slice(h * HALF, (h + 1) * HALF)
+            for m in range(MT):
+                if h == 1 and m % 2 == 0:
+                    nc.vector.tensor_copy(res[h][:, m, :], acc[m, h][:])
+                else:
+                    nc.scalar.copy(res[h][:, m, :], acc[m, h][:])
+                nc.sync.dma_start(out_v[:, m, cols], res[h][:, m, :])

@@ -16,8 +16,8 @@ MULT = mybir.AluOpType.mult
 
 P = 128
 PASSES = K // (4 * P)
-HALF = S // 2
-LIST_COLS = HALF // 16
+CH = 128
+CHUNKS = S // CH
 MT = M // P
 
 
@@ -66,86 +66,125 @@ def tile_list_heads_none_kernel(tc, xT, w_words, w_scales, wgt, offs, out):
         load_w(1)
         load_w(2)
 
+        last = PASSES - 1
         g, xb, codes, scales = {}, {}, {}, {}
-        for a in range(PASSES):
-            for h in range(2):
-                g[a, h] = keep.tile([P, 4, HALF], F32, name="g%d%d" % (a, h))
-                xb[a, h] = keep.tile([P, HALF, 4], BF16, name="xb%d%d" % (a, h), align_bytes=64)
-                codes[a, h] = keep.tile([P, HALF], U32, name="codes%d%d" % (a, h), align_bytes=64)
-                scales[a, h] = keep.tile([P, HALF], U8, name="scales%d%d" % (a, h), align_bytes=64)
-        acc = {}
-        for h in range(2):
-            for m in range(MT):
-                acc[m, h] = psum.tile([P, HALF], F32, name="acc%d%d" % (m, h))
+        for a in range(last):
+            g[a] = keep.tile([P, 4, S], F32, name="g%d" % a)
+            xb[a] = keep.tile([P, S, 4], BF16, name="xb%d" % a, align_bytes=64)
+            codes[a] = keep.tile([P, S], U32, name="codes%d" % a, align_bytes=64)
+            scales[a] = keep.tile([P, S], U8, name="scales%d" % a, align_bytes=64)
+        g_low = keep.tile([P, 3, S], F32, name="g_low")
+        g_end = [keep.tile([P, CH], F32, name="g_end%d" % i) for i in range(2)]
+        xb_last, codes_last, scales_last, acc = {}, {}, {}, {}
+        for c in range(CHUNKS):
+            xb_last[c] = keep.tile([P, CH, 4], BF16, name="xb_last%d" % c, align_bytes=64)
+            codes_last[c] = keep.tile([P, CH], U32, name="codes_last%d" % c, align_bytes=64)
+            scales_last[c] = keep.tile([P, CH], U8, name="scales_last%d" % c, align_bytes=64)
+            for mp in range(2):
+                acc[c, mp] = psum.tile([P, 2, CH], F32, name="acc%d%d" % (c, mp))
 
-        def gather(a, t, h, c0=0, c1=HALF):
-            j0, j1 = h * HALF + c0, h * HALF + c1
+        def gather(dst, a, t, j0, j1):
             nc.vector.tensor_tensor(
-                g[a, h][:, t, c0:c1],
+                dst,
                 x_sb[a, t][:].indirect(offsets[:, j0 // 16 : j1 // 16]),
                 wgt_sb[:, j0:j1],
                 MULT,
             )
 
-        def interleave(copy, a, h, t0, t1, c0=0, c1=HALF):
-            copy(xb[a, h][:, c0:c1, t0:t1], g[a, h][:, t0:t1, c0:c1].rearrange("p t n -> p n t"))
+        def interleave(copy, dst, src):
+            copy(dst, src.rearrange("p t n -> p n t"))
 
-        def quantize(a, h):
+        def quantize(words, plane, values):
             nc.vector.quantize_mx(
-                out=codes[a, h][:].bitcast(FP8X4),
-                scales=scales[a, h][:],
-                in_=xb[a, h][:].rearrange("p n t -> p (n t)"),
+                out=words[:].bitcast(FP8X4),
+                scales=plane[:],
+                in_=values[:].rearrange("p n t -> p (n t)"),
             )
 
-        def multiply(a, h):
+        def multiply(a, c):
+            if a == last:
+                words, plane = codes_last[c][:], scales_last[c][:]
+            else:
+                words, plane = codes[a][:, c * CH : (c + 1) * CH], scales[a][:, c * CH : (c + 1) * CH]
             for m in range(MT):
                 cols = slice(m * P, (m + 1) * P)
                 nc.tensor.matmul_mx(
-                    out=acc[m, h][:],
+                    out=acc[c, m // 2][:, m % 2, :],
                     lhsT=w_sb[a][:, cols].bitcast(FP8X4),
                     lhsT_scale=w_planes[4 * a : P, cols],
-                    rhs=codes[a, h][:].bitcast(FP8X4),
-                    rhs_scale=scales[a, h][:],
-                    start=(a == 0),
-                    stop=(a == PASSES - 1),
+                    rhs=words.bitcast(FP8X4),
+                    rhs_scale=plane,
+                    start=(a == 0 and m % 2 == 0),
+                    stop=(a == last and m % 2 == 1),
                 )
 
-        last = PASSES - 1
-        for a in range(PASSES):
-            for t in range(3 if a == last else 4):
-                for h in range(2):
-                    gather(a, t, h)
+        for a in range(last):
+            for t in range(4):
+                gather(g[a][:, t, :], a, t, 0, S)
                 if t == 0 and a > 0:
-                    for h in range(2):
-                        quantize(a - 1, h)
-                        multiply(a - 1, h)
-                if a == last and t == 1:
-                    for h in range(2):
-                        interleave(nc.scalar.copy, a, h, 0, 2)
-            if a < last:
-                for h in range(2):
-                    interleave(nc.scalar.copy, a, h, 0, 4)
+                    quantize(codes[a - 1], scales[a - 1], xb[a - 1])
+            interleave(nc.scalar.copy, xb[a][:], g[a][:])
+        gather(g_low[:, 0, :], last, 0, 0, S)
+        quantize(codes[last - 1], scales[last - 1], xb[last - 1])
+        gather(g_low[:, 1, :], last, 1, 0, S)
+        gather(g_low[:, 2, :], last, 2, 0, S)
+        caster = [nc.scalar.copy, nc.scalar.copy, nc.vector.tensor_copy, nc.vector.tensor_copy]
+        for c in range(CHUNKS):
+            interleave(nc.scalar.copy, xb_last[c][:, :, 0:2], g_low[:, 0:2, c * CH : (c + 1) * CH])
+        for c in range(CHUNKS):
+            caster[c](xb_last[c][:, :, 2], g_low[:, 2, c * CH : (c + 1) * CH])
+        for c in range(CHUNKS):
+            multiply(0, c)
 
         out_v = out.rearrange("(m p) j -> p m j", p=P)
-        res = [keep.tile([P, MT, HALF], F32, name="res%d" % h, align_bytes=256) for h in range(2)]
-        mid = HALF // 2
-        gather(last, 3, 0, 0, mid)
-        interleave(nc.scalar.copy, last, 0, 2, 4, 0, mid)
-        gather(last, 3, 0, mid, HALF)
-        gather(last, 3, 1, 0, mid)
-        interleave(nc.scalar.copy, last, 1, 2, 4, 0, mid)
-        interleave(nc.vector.tensor_copy, last, 0, 2, 4, mid, HALF)
-        quantize(last, 0)
+        res = [keep.tile([P, MT, CH], F32, name="res%d" % c, align_bytes=256) for c in range(CHUNKS)]
+
+        def last_gather(c):
+            gather(g_end[c % 2][:], last, 3, c * CH, (c + 1) * CH)
+
+        def cast(c):
+            caster[c](xb_last[c][:, :, 3], g_end[c % 2][:])
+
+        def last_quantize(c):
+            quantize(codes_last[c], scales_last[c], xb_last[c])
+
+        def evacuate(copy, c, mp):
+            copy(res[c][:, 2 * mp : 2 * mp + 2, :], acc[c, mp][:])
+
+        def store(c, m0, m1):
+            nc.sync.dma_start(out_v[:, m0:m1, c * CH : (c + 1) * CH], res[c][:, m0:m1, :])
+
+        last_gather(0)
+        cast(0)
+        last_gather(1)
+        cast(1)
+        multiply(1, 0)
+        last_quantize(0)
         multiply(last, 0)
-        gather(last, 3, 1, mid, HALF)
-        interleave(nc.vector.tensor_copy, last, 1, 2, 4, mid, HALF)
-        quantize(last, 1)
+        last_gather(2)
+        multiply(1, 1)
+        last_quantize(1)
         multiply(last, 1)
-        for h in range(2):
-            cols = slice(h * HALF, (h + 1) * HALF)
-            for m in range(MT):
-                if h == 1 and m % 2 == 0:
-                    nc.vector.tensor_copy(res[h][:, m, :], acc[m, h][:])
-                else:
-                    nc.scalar.copy(res[h][:, m, :], acc[m, h][:])
-                nc.sync.dma_start(out_v[:, m, cols], res[h][:, m, :])
+        last_gather(3)
+        evacuate(nc.scalar.copy, 0, 0)
+        store(0, 0, 2)
+        evacuate(nc.scalar.copy, 0, 1)
+        store(0, 2, 4)
+        cast(2)
+        cast(3)
+        multiply(1, 2)
+        multiply(1, 3)
+        last_quantize(2)
+        multiply(last, 2)
+        last_quantize(3)
+        multiply(last, 3)
+        evacuate(nc.scalar.copy, 1, 0)
+        evacuate(nc.scalar.copy, 1, 1)
+        store(1, 0, 4)
+        evacuate(nc.vector.tensor_copy, 2, 0)
+        evacuate(nc.scalar.copy, 2, 1)
+        store(2, 0, 4)
+        evacuate(nc.vector.tensor_copy, 3, 0)
+        store(3, 0, 2)
+        evacuate(nc.scalar.copy, 3, 1)
+        store(3, 2, 4)

@@ -48,36 +48,33 @@ def tile_list_heads_none_kernel(tc, xT, w_words, w_scales, wgt, offs, out):
                 w_scales[:, 4 * q : 4 * q + 4, :].bitcast(I32),
             )
 
-        w_sb = [keep.tile([P, M], I32, name="w_sb%d" % a, align_bytes=256) for a in range(PASSES)]
-
-        def load_w(a):
-            nc.sync.dma_start(w_sb[a][:], w_words[a].rearrange("p n t -> p (n t)").bitcast(I32))
+        w_first = keep.tile([P, M], I32, name="w_first", align_bytes=256)
+        w_rest = [keep.tile([P, PASSES - 1, M // 2], I32, name="w_rest%d" % mp, align_bytes=256) for mp in range(2)]
+        w_view = w_words.rearrange("a p n t -> p a (n t)").bitcast(I32)
 
         x_sb = {}
         for a in range(PASSES):
             rows = xT[4 * P * a : 4 * P * (a + 1), :].rearrange("(p t) c -> p t c", t=4)
             for t in range(4):
-                x_sb[a, t] = keep.tile([P, T], F32, name="x%d%d" % (a, t), align_bytes=256)
+                x_sb[a, t] = keep.tile([P, T], F32, name="x%d%d" % (a, t), tag="x%d%d" % (a, t), align_bytes=256)
                 if (a, t) == (2, 3):
-                    load_w(0)
+                    nc.sync.dma_start(w_first[:], w_view[:, 0, :])
                 nc.sync.dma_start(x_sb[a, t][:], rows[:, t, :])
                 if (a, t) == (0, 0):
                     nc.sync.dma_start(offsets[:], offs)
-        load_w(1)
-        load_w(2)
+        for mp in range(2):
+            nc.sync.dma_start(w_rest[mp][:], w_view[:, 1:, mp * M // 2 : (mp + 1) * M // 2])
 
         last = PASSES - 1
         g, xb, codes, scales = {}, {}, {}, {}
         for a in range(last):
             g[a] = keep.tile([P, 4, S], F32, name="g%d" % a)
             xb[a] = keep.tile([P, S, 4], BF16, name="xb%d" % a, align_bytes=64)
-            codes[a] = keep.tile([P, S], U32, name="codes%d" % a, align_bytes=64)
             scales[a] = keep.tile([P, S], U8, name="scales%d" % a, align_bytes=64)
-        g_low = keep.tile([P, 3, S], F32, name="g_low")
-        g_end = [keep.tile([P, CH], F32, name="g_end%d" % i) for i in range(2)]
+        g_head = keep.tile([P, 4, 3 * CH], F32, name="g_head")
+        g_tail = keep.tile([P, 4, CH], F32, name="g_tail")
         xb_last, codes_last, scales_last, acc = {}, {}, {}, {}
         for c in range(CHUNKS):
-            xb_last[c] = keep.tile([P, CH, 4], BF16, name="xb_last%d" % c, align_bytes=64)
             codes_last[c] = keep.tile([P, CH], U32, name="codes_last%d" % c, align_bytes=64)
             scales_last[c] = keep.tile([P, CH], U8, name="scales_last%d" % c, align_bytes=64)
             for mp in range(2):
@@ -101,16 +98,17 @@ def tile_list_heads_none_kernel(tc, xT, w_words, w_scales, wgt, offs, out):
                 in_=values[:].rearrange("p n t -> p (n t)"),
             )
 
-        def multiply(a, c):
+        def multiply(a, c, mp):
             if a == last:
                 words, plane = codes_last[c][:], scales_last[c][:]
             else:
                 words, plane = codes[a][:, c * CH : (c + 1) * CH], scales[a][:, c * CH : (c + 1) * CH]
-            for m in range(MT):
+            for m in (2 * mp, 2 * mp + 1):
                 cols = slice(m * P, (m + 1) * P)
+                w_codes = w_first[:, cols] if a == 0 else w_rest[mp][:, a - 1, (m % 2) * P : (m % 2 + 1) * P]
                 nc.tensor.matmul_mx(
                     out=acc[c, m // 2][:, m % 2, :],
-                    lhsT=w_sb[a][:, cols].bitcast(FP8X4),
+                    lhsT=w_codes.bitcast(FP8X4),
                     lhsT_scale=w_planes[4 * a : P, cols],
                     rhs=words.bitcast(FP8X4),
                     rhs_scale=plane,
@@ -118,32 +116,29 @@ def tile_list_heads_none_kernel(tc, xT, w_words, w_scales, wgt, offs, out):
                     stop=(a == last and m % 2 == 1),
                 )
 
+        def early_quantize(a, spent):
+            codes[a] = keep.tile([P, S], U32, name="codes%d" % a, tag="x%d%d" % spent, align_bytes=256)
+            quantize(codes[a], scales[a], xb[a])
+
         for a in range(last):
             for t in range(4):
                 gather(g[a][:, t, :], a, t, 0, S)
-                if t == 0 and a > 0:
-                    quantize(codes[a - 1], scales[a - 1], xb[a - 1])
+                if t == 1 and a > 0:
+                    early_quantize(a - 1, (a, t))
             interleave(nc.scalar.copy, xb[a][:], g[a][:])
-        gather(g_low[:, 0, :], last, 0, 0, S)
-        quantize(codes[last - 1], scales[last - 1], xb[last - 1])
-        gather(g_low[:, 1, :], last, 1, 0, S)
-        gather(g_low[:, 2, :], last, 2, 0, S)
-        caster = [nc.scalar.copy, nc.scalar.copy, nc.vector.tensor_copy, nc.vector.tensor_copy]
+        for t in range(3):
+            gather(g_head[:, t, :], last, t, 0, 3 * CH)
+            gather(g_tail[:, t, :], last, t, 3 * CH, S)
+        early_quantize(last - 1, (last, 2))
+        for c in range(2):
+            xb_last[c] = keep.tile([P, CH, 4], BF16, name="xb_last%d" % c, tag="xb_last%d" % c, align_bytes=64)
+            interleave(nc.scalar.copy, xb_last[c][:, :, 0:3], g_head[:, 0:3, c * CH : (c + 1) * CH])
         for c in range(CHUNKS):
-            interleave(nc.scalar.copy, xb_last[c][:, :, 0:2], g_low[:, 0:2, c * CH : (c + 1) * CH])
-        for c in range(CHUNKS):
-            caster[c](xb_last[c][:, :, 2], g_low[:, 2, c * CH : (c + 1) * CH])
-        for c in range(CHUNKS):
-            multiply(0, c)
+            for mp in range(2):
+                multiply(0, c, mp)
 
         out_v = out.rearrange("(m p) j -> p m j", p=P)
         res = [keep.tile([P, MT, CH], F32, name="res%d" % c, align_bytes=256) for c in range(CHUNKS)]
-
-        def last_gather(c):
-            gather(g_end[c % 2][:], last, 3, c * CH, (c + 1) * CH)
-
-        def cast(c):
-            caster[c](xb_last[c][:, :, 3], g_end[c % 2][:])
 
         def last_quantize(c):
             quantize(codes_last[c], scales_last[c], xb_last[c])
@@ -154,37 +149,36 @@ def tile_list_heads_none_kernel(tc, xT, w_words, w_scales, wgt, offs, out):
         def store(c, m0, m1):
             nc.sync.dma_start(out_v[:, m0:m1, c * CH : (c + 1) * CH], res[c][:, m0:m1, :])
 
-        last_gather(0)
-        cast(0)
-        last_gather(1)
-        cast(1)
-        multiply(1, 0)
+        gather(g_tail[:, 3, :], last, 3, 0, CH)
+        nc.scalar.copy(xb_last[0][:, :, 3], g_tail[:, 3, :])
+        gather(g_head[:, 3, CH : 2 * CH], last, 3, CH, 2 * CH)
+        nc.scalar.copy(xb_last[1][:, :, 3], g_head[:, 3, CH : 2 * CH])
+        gather(g_head[:, 3, 2 * CH :], last, 3, 2 * CH, 3 * CH)
+        for c in range(CHUNKS):
+            multiply(1, c, 0)
         last_quantize(0)
-        multiply(last, 0)
-        last_gather(2)
-        multiply(1, 1)
+        multiply(last, 0, 0)
+        multiply(1, 0, 1)
+        multiply(last, 0, 1)
+        gather(g_tail[:, 3, :], last, 3, 3 * CH, S)
         last_quantize(1)
-        multiply(last, 1)
-        last_gather(3)
-        evacuate(nc.scalar.copy, 0, 0)
-        store(0, 0, 2)
-        evacuate(nc.scalar.copy, 0, 1)
-        store(0, 2, 4)
-        cast(2)
-        cast(3)
-        multiply(1, 2)
-        multiply(1, 3)
-        last_quantize(2)
-        multiply(last, 2)
-        last_quantize(3)
-        multiply(last, 3)
-        evacuate(nc.scalar.copy, 1, 0)
-        evacuate(nc.scalar.copy, 1, 1)
-        store(1, 0, 4)
-        evacuate(nc.vector.tensor_copy, 2, 0)
-        evacuate(nc.scalar.copy, 2, 1)
-        store(2, 0, 4)
-        evacuate(nc.vector.tensor_copy, 3, 0)
-        store(3, 0, 2)
-        evacuate(nc.scalar.copy, 3, 1)
-        store(3, 2, 4)
+        for c in range(1, CHUNKS):
+            multiply(1, c, 1)
+        multiply(last, 1, 0)
+        multiply(last, 1, 1)
+        xb_last[2] = keep.tile([P, CH, 4], BF16, name="xb_last2", tag="xb_last0", align_bytes=64)
+        interleave(nc.vector.tensor_copy, xb_last[2][:], g_head[:, :, 2 * CH :])
+        xb_last[3] = keep.tile([P, CH, 4], BF16, name="xb_last3", tag="xb_last3", align_bytes=64)
+        interleave(nc.vector.tensor_copy, xb_last[3][:], g_tail[:])
+        for c in (2, 3):
+            last_quantize(c)
+            multiply(last, c, 0)
+            multiply(last, c, 1)
+        for c in range(CHUNKS):
+            for mp in range(2):
+                on_vector = (c, mp) in ((2, 1), (3, 0))
+                evacuate(nc.vector.tensor_copy if on_vector else nc.scalar.copy, c, mp)
+                if c < 2:
+                    store(c, 2 * mp, 2 * mp + 2)
+            if c >= 2:
+                store(c, 0, MT)

@@ -48,7 +48,7 @@ def tile_list_heads_none_kernel(tc, xT, w_words, w_scales, wgt, offs, out):
                 w_scales[:, 4 * q : 4 * q + 4, :].bitcast(I32),
             )
 
-        w_first = keep.tile([P, M], I32, name="w_first", align_bytes=256)
+        w_first = [keep.tile([P, M // 2], I32, name="w_first%d" % mp, align_bytes=256) for mp in range(2)]
         w_rest = [keep.tile([P, PASSES - 1, M // 2], I32, name="w_rest%d" % mp, align_bytes=256) for mp in range(2)]
         w_view = w_words.rearrange("a p n t -> p a (n t)").bitcast(I32)
 
@@ -58,10 +58,11 @@ def tile_list_heads_none_kernel(tc, xT, w_words, w_scales, wgt, offs, out):
             for t in range(4):
                 x_sb[a, t] = keep.tile([P, T], F32, name="x%d%d" % (a, t), tag="x%d%d" % (a, t), align_bytes=256)
                 if (a, t) == (2, 3):
-                    nc.sync.dma_start(w_first[:], w_view[:, 0, :])
+                    nc.sync.dma_start(w_first[0][:], w_view[:, 0, : M // 2])
                 nc.sync.dma_start(x_sb[a, t][:], rows[:, t, :])
                 if (a, t) == (0, 0):
                     nc.sync.dma_start(offsets[:], offs)
+        nc.sync.dma_start(w_first[1][:], w_view[:, 0, M // 2 :])
         for mp in range(2):
             nc.sync.dma_start(w_rest[mp][:], w_view[:, 1:, mp * M // 2 : (mp + 1) * M // 2])
 
@@ -78,7 +79,7 @@ def tile_list_heads_none_kernel(tc, xT, w_words, w_scales, wgt, offs, out):
             codes_last[c] = keep.tile([P, CH], U32, name="codes_last%d" % c, align_bytes=64)
             scales_last[c] = keep.tile([P, CH], U8, name="scales_last%d" % c, align_bytes=64)
             for mp in range(2):
-                acc[c, mp] = psum.tile([P, 2, CH], F32, name="acc%d%d" % (c, mp))
+                acc[c, mp] = psum.tile([P, 4, CH], F32, name="acc%d%d" % (c, mp))
 
         def gather(dst, a, t, j0, j1):
             nc.vector.tensor_tensor(
@@ -105,15 +106,17 @@ def tile_list_heads_none_kernel(tc, xT, w_words, w_scales, wgt, offs, out):
                 words, plane = codes[a][:, c * CH : (c + 1) * CH], scales[a][:, c * CH : (c + 1) * CH]
             for m in (2 * mp, 2 * mp + 1):
                 cols = slice(m * P, (m + 1) * P)
-                w_codes = w_first[:, cols] if a == 0 else w_rest[mp][:, a - 1, (m % 2) * P : (m % 2 + 1) * P]
+                bank, slot = (mp, m % 2) if c == 0 else (m % 2, mp)
+                half = slice((m % 2) * P, (m % 2 + 1) * P)
+                w_codes = w_first[mp][:, half] if a == 0 else w_rest[mp][:, a - 1, half]
                 nc.tensor.matmul_mx(
-                    out=acc[c, m // 2][:, m % 2, :],
+                    out=acc[c, bank][:, slot, :],
                     lhsT=w_codes.bitcast(FP8X4),
                     lhsT_scale=w_planes[4 * a : P, cols],
                     rhs=words.bitcast(FP8X4),
                     rhs_scale=plane,
-                    start=(a == 0 and m % 2 == 0),
-                    stop=(a == last and m % 2 == 1),
+                    start=(a == 0 and slot == 0),
+                    stop=(a == last and slot == 1),
                 )
 
         def early_quantize(a, spent):
@@ -130,11 +133,21 @@ def tile_list_heads_none_kernel(tc, xT, w_words, w_scales, wgt, offs, out):
             gather(g_head[:, t, :], last, t, 0, 3 * CH)
             gather(g_tail[:, t, :], last, t, 3 * CH, S)
         early_quantize(last - 1, (last, 2))
-        for c in range(2):
+        for c in range(3):
             xb_last[c] = keep.tile([P, CH, 4], BF16, name="xb_last%d" % c, tag="xb_last%d" % c, align_bytes=64)
             interleave(nc.scalar.copy, xb_last[c][:, :, 0:3], g_head[:, 0:3, c * CH : (c + 1) * CH])
-        for c in range(CHUNKS):
-            for mp in range(2):
+        for c in range(2):
+            nc.tensor.matmul_mx(
+                out=acc[c, 1][0:32].rearrange("p m j -> p (m j)"),
+                lhsT=w_first[0][:, 0:32].bitcast(FP8X4),
+                lhsT_scale=w_planes[:, 0:32],
+                rhs=codes[0][:].bitcast(FP8X4),
+                rhs_scale=scales[0][:],
+                start=True,
+                stop=True,
+            )
+        for mp in range(2):
+            for c in range(CHUNKS):
                 multiply(0, c, mp)
 
         out_v = out.rearrange("(m p) j -> p m j", p=P)
@@ -143,42 +156,47 @@ def tile_list_heads_none_kernel(tc, xT, w_words, w_scales, wgt, offs, out):
         def last_quantize(c):
             quantize(codes_last[c], scales_last[c], xb_last[c])
 
-        def evacuate(copy, c, mp):
-            copy(res[c][:, 2 * mp : 2 * mp + 2, :], acc[c, mp][:])
+        def held(c, bank):
+            return slice(2 * bank, 2 * bank + 2) if c == 0 else slice(bank, MT, 2)
 
-        def store(c, m0, m1):
-            nc.sync.dma_start(out_v[:, m0:m1, c * CH : (c + 1) * CH], res[c][:, m0:m1, :])
+        def evacuate(copy, c, mp):
+            copy(res[c][:, held(c, mp), :], acc[c, mp][:, 0:2, :])
+
+        def store(c, tiles):
+            nc.sync.dma_start(out_v[:, tiles, c * CH : (c + 1) * CH], res[c][:, tiles, :])
 
         gather(g_tail[:, 3, :], last, 3, 0, CH)
         nc.scalar.copy(xb_last[0][:, :, 3], g_tail[:, 3, :])
         gather(g_head[:, 3, CH : 2 * CH], last, 3, CH, 2 * CH)
         nc.scalar.copy(xb_last[1][:, :, 3], g_head[:, 3, CH : 2 * CH])
         gather(g_head[:, 3, 2 * CH :], last, 3, 2 * CH, 3 * CH)
-        for c in range(CHUNKS):
-            multiply(1, c, 0)
+        nc.scalar.copy(xb_last[2][:, :, 3], g_head[:, 3, 2 * CH :])
+        multiply(1, 0, 0)
+        multiply(1, 1, 0)
         last_quantize(0)
         multiply(last, 0, 0)
+        multiply(1, 2, 0)
+        multiply(1, 3, 0)
         multiply(1, 0, 1)
         multiply(last, 0, 1)
         gather(g_tail[:, 3, :], last, 3, 3 * CH, S)
         last_quantize(1)
-        for c in range(1, CHUNKS):
-            multiply(1, c, 1)
+        multiply(1, 1, 1)
         multiply(last, 1, 0)
         multiply(last, 1, 1)
-        xb_last[2] = keep.tile([P, CH, 4], BF16, name="xb_last2", tag="xb_last0", align_bytes=64)
-        interleave(nc.vector.tensor_copy, xb_last[2][:], g_head[:, :, 2 * CH :])
         xb_last[3] = keep.tile([P, CH, 4], BF16, name="xb_last3", tag="xb_last3", align_bytes=64)
         interleave(nc.vector.tensor_copy, xb_last[3][:], g_tail[:])
         for c in (2, 3):
             last_quantize(c)
+            multiply(1, c, 1)
             multiply(last, c, 0)
             multiply(last, c, 1)
         for c in range(CHUNKS):
+            whole = c >= 2
             for mp in range(2):
-                on_vector = (c, mp) in ((2, 1), (3, 0))
+                on_vector = (c, mp) in ((1, 1), (2, 1), (3, 1))
                 evacuate(nc.vector.tensor_copy if on_vector else nc.scalar.copy, c, mp)
-                if c < 2:
-                    store(c, 2 * mp, 2 * mp + 2)
-            if c >= 2:
-                store(c, 0, MT)
+                if not whole:
+                    store(c, held(c, mp))
+            if whole:
+                store(c, slice(0, MT))

@@ -54,12 +54,15 @@ def tile_list_heads_none_kernel(tc, xT, w_words, w_scales, wgt, offs, out):
 
         x_sb = {}
         for a in range(PASSES):
-            rows = xT[4 * P * a : 4 * P * (a + 1), :].rearrange("(p t) c -> p t c", t=4)
+            rows = xT[4 * P * a : 4 * P * (a + 1), :].rearrange("(p t) c -> p (t c)", t=4)
             for t in range(4):
-                x_sb[a, t] = keep.tile([P, T], F32, name="x%d%d" % (a, t), tag="x%d%d" % (a, t), align_bytes=256)
+                paired = a < PASSES - 1
+                width = 2 * T if paired and t % 2 == 0 else T
+                x_sb[a, t] = keep.tile([P, width], F32, name="x%d%d" % (a, t), tag="x%d%d" % (a, t), align_bytes=256)
                 if (a, t) == (2, 3):
                     nc.sync.dma_start(w_first[0][:], w_view[:, 0, : M // 2])
-                nc.sync.dma_start(x_sb[a, t][:], rows[:, t, :])
+                if not (paired and t % 2 == 1):
+                    nc.sync.dma_start(x_sb[a, t][:], rows[:, t * T : t * T + width])
                 if (a, t) == (0, 0):
                     nc.sync.dma_start(offsets[:], offs)
         nc.sync.dma_start(w_first[1][:], w_view[:, 0, M // 2 :])
@@ -125,10 +128,15 @@ def tile_list_heads_none_kernel(tc, xT, w_words, w_scales, wgt, offs, out):
 
         for a in range(last):
             for t in range(4):
-                gather(g[a][:, t, :], a, t, 0, S)
-                if t == 1 and a > 0:
-                    early_quantize(a - 1, (a, t))
-            interleave(nc.scalar.copy, xb[a][:], g[a][:])
+                if t % 2 == 0:
+                    nc.scalar.copy(x_sb[a, t + 1][:], x_sb[a, t][:, T:])
+                    gather(g[a][:, t, : S // 2], a, t, 0, S // 2)
+                    gather(g[a][:, t, S // 2 :], a, t, S // 2, S)
+                else:
+                    gather(g[a][:, t, :], a, t, 0, S)
+            interleave(nc.vector.tensor_copy if a == 0 else nc.scalar.copy, xb[a][:], g[a][:])
+            if a == 0:
+                early_quantize(0, (0, 3))
         for t in range(3):
             gather(g_head[:, t, :], last, t, 0, 3 * CH)
             gather(g_tail[:, t, :], last, t, 3 * CH, S)

@@ -48,9 +48,15 @@ def tile_list_heads_none_kernel(tc, xT, w_words, w_scales, wgt, offs, out):
                 w_scales[:, 4 * q : 4 * q + 4, :].bitcast(I32),
             )
 
-        w_first = [keep.tile([P, M // 2], I32, name="w_first%d" % mp, align_bytes=256) for mp in range(2)]
-        w_rest = [keep.tile([P, PASSES - 1, M // 2], I32, name="w_rest%d" % mp, align_bytes=256) for mp in range(2)]
         w_view = w_words.rearrange("a p n t -> p a (n t)").bitcast(I32)
+        w_sb = {}
+
+        def load_weights(a0, a1, m0, m1):
+            words = keep.tile([P, a1 - a0, (m1 - m0) * P], I32, name="w%d%d" % (a0, m0), align_bytes=256)
+            nc.sync.dma_start(words[:], w_view[:, a0:a1, m0 * P : m1 * P])
+            for a in range(a0, a1):
+                for m in range(m0, m1):
+                    w_sb[a, m] = words[:, a - a0, (m - m0) * P : (m - m0 + 1) * P]
 
         x_sb = {}
         for a in range(PASSES):
@@ -60,14 +66,13 @@ def tile_list_heads_none_kernel(tc, xT, w_words, w_scales, wgt, offs, out):
                 width = 2 * T if paired and t % 2 == 0 else T
                 x_sb[a, t] = keep.tile([P, width], F32, name="x%d%d" % (a, t), tag="x%d%d" % (a, t), align_bytes=256)
                 if (a, t) == (2, 3):
-                    nc.sync.dma_start(w_first[0][:], w_view[:, 0, : M // 2])
+                    load_weights(0, 1, 0, 2)
                 if not (paired and t % 2 == 1):
                     nc.sync.dma_start(x_sb[a, t][:], rows[:, t * T : t * T + width])
                 if (a, t) == (0, 0):
                     nc.sync.dma_start(offsets[:], offs)
-        nc.sync.dma_start(w_first[1][:], w_view[:, 0, M // 2 :])
-        for mp in range(2):
-            nc.sync.dma_start(w_rest[mp][:], w_view[:, 1:, mp * M // 2 : (mp + 1) * M // 2])
+        for a0, a1, m0, m1 in ((0, 1, 2, 3), (0, 1, 3, 4), (1, 3, 0, 1), (1, 3, 1, 2), (1, 3, 2, 4)):
+            load_weights(a0, a1, m0, m1)
 
         last = PASSES - 1
         g, xb, codes, scales = {}, {}, {}, {}
@@ -110,11 +115,9 @@ def tile_list_heads_none_kernel(tc, xT, w_words, w_scales, wgt, offs, out):
             for m in (2 * mp, 2 * mp + 1):
                 cols = slice(m * P, (m + 1) * P)
                 bank, slot = (mp, m % 2) if c == 0 else (m % 2, mp)
-                half = slice((m % 2) * P, (m % 2 + 1) * P)
-                w_codes = w_first[mp][:, half] if a == 0 else w_rest[mp][:, a - 1, half]
                 nc.tensor.matmul_mx(
                     out=acc[c, bank][:, slot, :],
-                    lhsT=w_codes.bitcast(FP8X4),
+                    lhsT=w_sb[a, m].bitcast(FP8X4),
                     lhsT_scale=w_planes[4 * a : P, cols],
                     rhs=words.bitcast(FP8X4),
                     rhs_scale=plane,
@@ -147,7 +150,7 @@ def tile_list_heads_none_kernel(tc, xT, w_words, w_scales, wgt, offs, out):
         for c in range(2):
             nc.tensor.matmul_mx(
                 out=acc[c, 1][0:32].rearrange("p m j -> p (m j)"),
-                lhsT=w_first[0][:, 0:32].bitcast(FP8X4),
+                lhsT=w_sb[0, 0][:, 0:32].bitcast(FP8X4),
                 lhsT_scale=w_planes[:, 0:32],
                 rhs=codes[0][:].bitcast(FP8X4),
                 rhs_scale=scales[0][:],
@@ -200,7 +203,7 @@ def tile_list_heads_none_kernel(tc, xT, w_words, w_scales, wgt, offs, out):
             multiply(last, c, 0)
             multiply(last, c, 1)
         for c in range(CHUNKS):
-            whole = c >= 2
+            whole = False
             for mp in range(2):
                 on_vector = (c, mp) in ((1, 1), (2, 1), (3, 1))
                 evacuate(nc.vector.tensor_copy if on_vector else nc.scalar.copy, c, mp)

@@ -107,14 +107,14 @@ def tile_list_heads_none_kernel(tc, xT, w_words, w_scales, wgt, offs, out):
                 in_=values[:].rearrange("p n t -> p (n t)"),
             )
 
-        def multiply(a, c, mp):
+        def multiply(a, c, tiles):
             if a == last:
                 words, plane = codes_last[c][:], scales_last[c][:]
             else:
                 words, plane = codes[a][:, c * CH : (c + 1) * CH], scales[a][:, c * CH : (c + 1) * CH]
-            for m in (2 * mp, 2 * mp + 1):
+            for m in tiles:
                 cols = slice(m * P, (m + 1) * P)
-                bank, slot = (mp, m % 2) if c == 0 else (m % 2, mp)
+                bank, slot = (m // 2, m % 2) if c == 0 else (m % 2, m // 2)
                 nc.tensor.matmul_mx(
                     out=acc[c, bank][:, slot, :],
                     lhsT=w_sb[a, m].bitcast(FP8X4),
@@ -159,7 +159,7 @@ def tile_list_heads_none_kernel(tc, xT, w_words, w_scales, wgt, offs, out):
             )
         for mp in range(2):
             for c in range(CHUNKS):
-                multiply(0, c, mp)
+                multiply(0, c, (2 * mp, 2 * mp + 1))
 
         out_v = out.rearrange("(m p) j -> p m j", p=P)
         res = [keep.tile([P, MT, CH], F32, name="res%d" % c, align_bytes=256) for c in range(CHUNKS)]
@@ -182,26 +182,26 @@ def tile_list_heads_none_kernel(tc, xT, w_words, w_scales, wgt, offs, out):
         nc.scalar.copy(xb_last[1][:, :, 3], g_head[:, 3, CH : 2 * CH])
         gather(g_head[:, 3, 2 * CH :], last, 3, 2 * CH, 3 * CH)
         nc.scalar.copy(xb_last[2][:, :, 3], g_head[:, 3, 2 * CH :])
-        multiply(1, 0, 0)
-        multiply(1, 1, 0)
+        for c in range(CHUNKS):
+            multiply(1, c, (0, 1) if c < 2 else (0,))
         last_quantize(0)
-        multiply(last, 0, 0)
-        multiply(1, 2, 0)
-        multiply(1, 3, 0)
-        multiply(1, 0, 1)
-        multiply(last, 0, 1)
+        multiply(last, 0, (0, 1))
+        multiply(1, 0, (2, 3))
+        multiply(last, 0, (2, 3))
+
+        def finish(c):
+            for bank in range(2):
+                multiply(1, c, (3, 1) if c >= 2 and bank == 1 else (2 + bank,))
+                multiply(last, c, (bank, 2 + bank))
+
         gather(g_tail[:, 3, :], last, 3, 3 * CH, S)
         last_quantize(1)
-        multiply(1, 1, 1)
-        multiply(last, 1, 0)
-        multiply(last, 1, 1)
+        finish(1)
         xb_last[3] = keep.tile([P, CH, 4], BF16, name="xb_last3", tag="xb_last3", align_bytes=64)
         interleave(nc.vector.tensor_copy, xb_last[3][:], g_tail[:])
         for c in (2, 3):
             last_quantize(c)
-            multiply(1, c, 1)
-            multiply(last, c, 0)
-            multiply(last, c, 1)
+            finish(c)
         for c in range(CHUNKS):
             whole = False
             for mp in range(2):

@@ -19,6 +19,7 @@ PASSES = K // (4 * P)
 CH = 128
 CHUNKS = S // CH
 MT = M // P
+HALF = S // 2
 
 
 def tile_list_heads_none_kernel(tc, xT, w_words, w_scales, wgt, offs, out):
@@ -62,32 +63,28 @@ def tile_list_heads_none_kernel(tc, xT, w_words, w_scales, wgt, offs, out):
         for a in range(PASSES):
             rows = xT[4 * P * a : 4 * P * (a + 1), :].rearrange("(p t) c -> p (t c)", t=4)
             for t in range(4):
-                paired = a < PASSES - 1
+                paired = a == 0
                 width = 2 * T if paired and t % 2 == 0 else T
                 x_sb[a, t] = keep.tile([P, width], F32, name="x%d%d" % (a, t), tag="x%d%d" % (a, t), align_bytes=256)
-                if (a, t) == (2, 3):
+                if (a, t) == (PASSES - 1, 3):
                     load_weights(0, 1, 0, 2)
                 if not (paired and t % 2 == 1):
                     nc.sync.dma_start(x_sb[a, t][:], rows[:, t * T : t * T + width])
                 if (a, t) == (0, 0):
                     nc.sync.dma_start(offsets[:], offs)
-        for a0, a1, m0, m1 in ((0, 1, 2, 3), (0, 1, 3, 4), (1, 3, 0, 1), (1, 3, 1, 2), (1, 3, 2, 4)):
+        for a0, a1, m0, m1 in ((0, 1, 2, 4), (1, 3, 0, 2), (1, 3, 2, 4)):
             load_weights(a0, a1, m0, m1)
 
         last = PASSES - 1
-        g, xb, codes, scales = {}, {}, {}, {}
-        for a in range(last):
-            g[a] = keep.tile([P, 4, S], F32, name="g%d" % a)
-            xb[a] = keep.tile([P, S, 4], BF16, name="xb%d" % a, align_bytes=64)
-            scales[a] = keep.tile([P, S], U8, name="scales%d" % a, align_bytes=64)
-        g_head = keep.tile([P, 4, 3 * CH], F32, name="g_head")
-        g_tail = keep.tile([P, 4, CH], F32, name="g_tail")
-        xb_last, codes_last, scales_last, acc = {}, {}, {}, {}
+        g = [keep.tile([P, 4, S], F32, name="g%d" % a) for a in range(last)]
+        g_low = keep.tile([P, 2, S], F32, name="g_low")
+        g_rows = keep.tile([P, CHUNKS + 3, CH], F32, name="g_rows")
+        g_high = [g_rows[:, c : CHUNKS + c % 3 + 1 : CHUNKS + c % 3 - c, :] for c in range(CHUNKS)]
+        acc = {}
         for c in range(CHUNKS):
-            codes_last[c] = keep.tile([P, CH], U32, name="codes_last%d" % c, align_bytes=64)
-            scales_last[c] = keep.tile([P, CH], U8, name="scales_last%d" % c, align_bytes=64)
-            for mp in range(2):
-                acc[c, mp] = psum.tile([P, 4, CH], F32, name="acc%d%d" % (c, mp))
+            for b in range(2):
+                acc[c, b] = psum.tile([P, 4, CH], F32, name="acc%d%d" % (c, b))
+        operand = {}
 
         def gather(dst, a, t, j0, j1):
             nc.vector.tensor_tensor(
@@ -100,114 +97,112 @@ def tile_list_heads_none_kernel(tc, xT, w_words, w_scales, wgt, offs, out):
         def interleave(copy, dst, src):
             copy(dst, src.rearrange("p t n -> p n t"))
 
-        def quantize(words, plane, values):
+        def quantize(a, c0, c1, values, tag):
+            width = (c1 - c0) * CH
+            words = keep.tile([P, width], U32, name="codes%d%d" % (a, c0), tag=tag, align_bytes=256)
+            plane = keep.tile([P, width], U8, name="scales%d%d" % (a, c0), align_bytes=64)
             nc.vector.quantize_mx(
                 out=words[:].bitcast(FP8X4),
                 scales=plane[:],
                 in_=values[:].rearrange("p n t -> p (n t)"),
             )
+            for c in range(c0, c1):
+                cols = slice((c - c0) * CH, (c - c0 + 1) * CH)
+                operand[a, c] = (words[:, cols], plane[:, cols])
+            return words, plane
+
+        def place(c, m):
+            return (m // 2, m % 2) if c == 0 else (m % 2, m // 2)
+
+        opened = set()
 
         def multiply(a, c, tiles):
-            if a == last:
-                words, plane = codes_last[c][:], scales_last[c][:]
-            else:
-                words, plane = codes[a][:, c * CH : (c + 1) * CH], scales[a][:, c * CH : (c + 1) * CH]
+            words, plane = operand[a, c]
             for m in tiles:
-                cols = slice(m * P, (m + 1) * P)
-                bank, slot = (m // 2, m % 2) if c == 0 else (m % 2, m // 2)
+                bank, slot = place(c, m)
                 nc.tensor.matmul_mx(
                     out=acc[c, bank][:, slot, :],
                     lhsT=w_sb[a, m].bitcast(FP8X4),
-                    lhsT_scale=w_planes[4 * a : P, cols],
+                    lhsT_scale=w_planes[4 * a : P, m * P : (m + 1) * P],
                     rhs=words.bitcast(FP8X4),
                     rhs_scale=plane,
-                    start=(a == 0 and slot == 0),
+                    start=(c, bank) not in opened,
                     stop=(a == last and slot == 1),
                 )
+                opened.add((c, bank))
 
-        def early_quantize(a, spent):
-            codes[a] = keep.tile([P, S], U32, name="codes%d" % a, tag="x%d%d" % spent, align_bytes=256)
-            quantize(codes[a], scales[a], xb[a])
-
+        xb = [keep.tile([P, S, 4], BF16, name="xb%d" % a, align_bytes=64) for a in range(last)]
+        xb2 = [keep.tile([P, CH, 4], BF16, name="xb2%d" % c, align_bytes=64) for c in range(CHUNKS)]
         for a in range(last):
             for t in range(4):
-                if t % 2 == 0:
+                if a == 0 and t % 2 == 0:
                     nc.scalar.copy(x_sb[a, t + 1][:], x_sb[a, t][:, T:])
-                    gather(g[a][:, t, : S // 2], a, t, 0, S // 2)
-                    gather(g[a][:, t, S // 2 :], a, t, S // 2, S)
+                    gather(g[a][:, t, :HALF], a, t, 0, HALF)
+                    gather(g[a][:, t, HALF:], a, t, HALF, S)
                 else:
                     gather(g[a][:, t, :], a, t, 0, S)
-            interleave(nc.vector.tensor_copy if a == 0 else nc.scalar.copy, xb[a][:], g[a][:])
-            if a == 0:
-                early_quantize(0, (0, 3))
-        for t in range(3):
-            gather(g_head[:, t, :], last, t, 0, 3 * CH)
-            gather(g_tail[:, t, :], last, t, 3 * CH, S)
-        early_quantize(last - 1, (last, 2))
-        for c in range(3):
-            xb_last[c] = keep.tile([P, CH, 4], BF16, name="xb_last%d" % c, tag="xb_last%d" % c, align_bytes=64)
-            interleave(nc.scalar.copy, xb_last[c][:, :, 0:3], g_head[:, 0:3, c * CH : (c + 1) * CH])
+                if (a, t) == (1, 1):
+                    words0, plane0 = quantize(0, 0, CHUNKS, xb[0], "x11")
+            interleave(nc.scalar.copy, xb[a][:], g[a][:])
+        for t in range(2):
+            gather(g_low[:, t, :], last, t, 0, S)
+        quantize(1, 0, CHUNKS, xb[1], "x21")
+        for c in range(CHUNKS):
+            interleave(nc.scalar.copy, xb2[c][:, :, 0:2], g_low[:, :, c * CH : (c + 1) * CH])
+        gather(g_rows[:, 0:CHUNKS, :].rearrange("p c n -> p (c n)"), last, 2, 0, S)
         for c in range(2):
             nc.tensor.matmul_mx(
                 out=acc[c, 1][0:32].rearrange("p m j -> p (m j)"),
                 lhsT=w_sb[0, 0][:, 0:32].bitcast(FP8X4),
                 lhsT_scale=w_planes[:, 0:32],
-                rhs=codes[0][:].bitcast(FP8X4),
-                rhs_scale=scales[0][:],
+                rhs=words0[:].bitcast(FP8X4),
+                rhs_scale=plane0[:],
                 start=True,
                 stop=True,
             )
-        for mp in range(2):
-            for c in range(CHUNKS):
-                multiply(0, c, (2 * mp, 2 * mp + 1))
 
         out_v = out.rearrange("(m p) j -> p m j", p=P)
         res = [keep.tile([P, MT, CH], F32, name="res%d" % c, align_bytes=256) for c in range(CHUNKS)]
 
-        def last_quantize(c):
-            quantize(codes_last[c], scales_last[c], xb_last[c])
-
         def held(c, bank):
             return slice(2 * bank, 2 * bank + 2) if c == 0 else slice(bank, MT, 2)
 
-        def evacuate(copy, c, mp):
-            copy(res[c][:, held(c, mp), :], acc[c, mp][:, 0:2, :])
+        def gather_last(c):
+            gather(g_high[c][:, 1, :], last, 3, c * CH, (c + 1) * CH)
 
-        def store(c, tiles):
+        def round_last(copy, c):
+            interleave(copy, xb2[c][:, :, 2:4], g_high[c])
+
+        def quantize_last(c):
+            quantize(last, c, c + 1, xb2[c], "codes_last%d" % c)
+
+        def leave(copy, c, bank):
+            tiles = held(c, bank)
+            copy(res[c][:, tiles, :], acc[c, bank][:, 0:2, :])
             nc.sync.dma_start(out_v[:, tiles, c * CH : (c + 1) * CH], res[c][:, tiles, :])
 
-        gather(g_tail[:, 3, :], last, 3, 0, CH)
-        nc.scalar.copy(xb_last[0][:, :, 3], g_tail[:, 3, :])
-        gather(g_head[:, 3, CH : 2 * CH], last, 3, CH, 2 * CH)
-        nc.scalar.copy(xb_last[1][:, :, 3], g_head[:, 3, CH : 2 * CH])
-        gather(g_head[:, 3, 2 * CH :], last, 3, 2 * CH, 3 * CH)
-        nc.scalar.copy(xb_last[2][:, :, 3], g_head[:, 3, 2 * CH :])
+        for c in range(3):
+            gather_last(c)
+            round_last(nc.scalar.copy, c)
+        quantize_last(0)
+        gather_last(3)
+        quantize_last(1)
+        round_last(nc.vector.tensor_copy, 3)
+        for c in (2, 3):
+            quantize_last(c)
+
+        for pair in ((0, 1), (2, 3)):
+            for c in range(CHUNKS):
+                multiply(0, c, pair)
         for c in range(CHUNKS):
             multiply(1, c, (0, 1) if c < 2 else (0,))
-        last_quantize(0)
         multiply(last, 0, (0, 1))
-        multiply(1, 0, (2, 3))
-        multiply(last, 0, (2, 3))
-
-        def finish(c):
+        leave(nc.scalar.copy, 0, 0)
+        for a in (1, last):
+            multiply(a, 0, (2, 3))
+        leave(nc.scalar.copy, 0, 1)
+        for c in range(1, CHUNKS):
             for bank in range(2):
                 multiply(1, c, (3, 1) if c >= 2 and bank == 1 else (2 + bank,))
                 multiply(last, c, (bank, 2 + bank))
-
-        gather(g_tail[:, 3, :], last, 3, 3 * CH, S)
-        last_quantize(1)
-        finish(1)
-        xb_last[3] = keep.tile([P, CH, 4], BF16, name="xb_last3", tag="xb_last3", align_bytes=64)
-        interleave(nc.vector.tensor_copy, xb_last[3][:], g_tail[:])
-        for c in (2, 3):
-            last_quantize(c)
-            finish(c)
-        for c in range(CHUNKS):
-            whole = False
-            for mp in range(2):
-                on_vector = (c, mp) in ((1, 1), (2, 1), (3, 1))
-                evacuate(nc.vector.tensor_copy if on_vector else nc.scalar.copy, c, mp)
-                if not whole:
-                    store(c, held(c, mp))
-            if whole:
-                store(c, slice(0, MT))
+                leave(nc.scalar.copy if bank == 0 else nc.vector.tensor_copy, c, bank)

@@ -16,6 +16,7 @@ MULT = mybir.AluOpType.mult
 
 P = 128
 PASSES = K // (4 * P)
+LAST = PASSES - 1
 CH = 128
 CHUNKS = S // CH
 MT = M // P
@@ -52,12 +53,11 @@ def tile_list_heads_none_kernel(tc, xT, w_words, w_scales, wgt, offs, out):
         w_view = w_words.rearrange("a p n t -> p a (n t)").bitcast(I32)
         w_sb = {}
 
-        def load_weights(a0, a1, m0, m1):
-            words = keep.tile([P, a1 - a0, (m1 - m0) * P], I32, name="w%d%d" % (a0, m0), align_bytes=256)
-            nc.sync.dma_start(words[:], w_view[:, a0:a1, m0 * P : m1 * P])
-            for a in range(a0, a1):
-                for m in range(m0, m1):
-                    w_sb[a, m] = words[:, a - a0, (m - m0) * P : (m - m0 + 1) * P]
+        def load_weights(a, m0, m1):
+            words = keep.tile([P, (m1 - m0) * P], I32, name="w%d%d" % (a, m0), align_bytes=256)
+            nc.sync.dma_start(words[:], w_view[:, a, m0 * P : m1 * P])
+            for m in range(m0, m1):
+                w_sb[a, m] = words[:, (m - m0) * P : (m - m0 + 1) * P]
 
         x_sb = {}
         for a in range(PASSES):
@@ -66,17 +66,17 @@ def tile_list_heads_none_kernel(tc, xT, w_words, w_scales, wgt, offs, out):
                 paired = a == 0
                 width = 2 * T if paired and t % 2 == 0 else T
                 x_sb[a, t] = keep.tile([P, width], F32, name="x%d%d" % (a, t), tag="x%d%d" % (a, t), align_bytes=256)
-                if (a, t) == (PASSES - 1, 3):
-                    load_weights(0, 1, 0, 2)
+                if (a, t) == (LAST, 3):
+                    load_weights(0, 0, MT)
                 if not (paired and t % 2 == 1):
                     nc.sync.dma_start(x_sb[a, t][:], rows[:, t * T : t * T + width])
                 if (a, t) == (0, 0):
                     nc.sync.dma_start(offsets[:], offs)
-        for a0, a1, m0, m1 in ((0, 1, 2, 4), (1, 3, 0, 2), (1, 3, 2, 4)):
-            load_weights(a0, a1, m0, m1)
+        load_weights(1, 0, 2)
+        load_weights(1, 2, MT)
+        load_weights(LAST, 0, MT)
 
-        last = PASSES - 1
-        g = [keep.tile([P, 4, S], F32, name="g%d" % a) for a in range(last)]
+        g = [keep.tile([P, 4, S], F32, name="g%d" % a) for a in range(LAST)]
         g_low = keep.tile([P, 2, S], F32, name="g_low")
         g_rows = keep.tile([P, CHUNKS + 3, CH], F32, name="g_rows")
         g_high = [g_rows[:, c : CHUNKS + c % 3 + 1 : CHUNKS + c % 3 - c, :] for c in range(CHUNKS)]
@@ -109,31 +109,24 @@ def tile_list_heads_none_kernel(tc, xT, w_words, w_scales, wgt, offs, out):
             for c in range(c0, c1):
                 cols = slice((c - c0) * CH, (c - c0 + 1) * CH)
                 operand[a, c] = (words[:, cols], plane[:, cols])
-            return words, plane
 
-        def place(c, m):
-            return (m // 2, m % 2) if c == 0 else (m % 2, m // 2)
-
-        opened = set()
-
-        def multiply(a, c, tiles):
+        def multiply(a, c, bank):
             words, plane = operand[a, c]
-            for m in tiles:
-                bank, slot = place(c, m)
+            for slot in range(2):
+                m = 2 * bank + slot
                 nc.tensor.matmul_mx(
                     out=acc[c, bank][:, slot, :],
                     lhsT=w_sb[a, m].bitcast(FP8X4),
                     lhsT_scale=w_planes[4 * a : P, m * P : (m + 1) * P],
                     rhs=words.bitcast(FP8X4),
                     rhs_scale=plane,
-                    start=(c, bank) not in opened,
-                    stop=(a == last and slot == 1),
+                    start=(a == 0 and slot == 0),
+                    stop=(a == LAST and slot == 1),
                 )
-                opened.add((c, bank))
 
-        xb = [keep.tile([P, S, 4], BF16, name="xb%d" % a, align_bytes=64) for a in range(last)]
+        xb = [keep.tile([P, S, 4], BF16, name="xb%d" % a, align_bytes=64) for a in range(LAST)]
         xb2 = [keep.tile([P, CH, 4], BF16, name="xb2%d" % c, align_bytes=64) for c in range(CHUNKS)]
-        for a in range(last):
+        for a in range(LAST):
             for t in range(4):
                 if a == 0 and t % 2 == 0:
                     nc.scalar.copy(x_sb[a, t + 1][:], x_sb[a, t][:, T:])
@@ -142,42 +135,29 @@ def tile_list_heads_none_kernel(tc, xT, w_words, w_scales, wgt, offs, out):
                 else:
                     gather(g[a][:, t, :], a, t, 0, S)
                 if (a, t) == (1, 1):
-                    words0, plane0 = quantize(0, 0, CHUNKS, xb[0], "x11")
+                    quantize(0, 0, CHUNKS, xb[0], "x11")
             interleave(nc.scalar.copy, xb[a][:], g[a][:])
         for t in range(2):
-            gather(g_low[:, t, :], last, t, 0, S)
+            gather(g_low[:, t, :], LAST, t, 0, S)
         quantize(1, 0, CHUNKS, xb[1], "x21")
         for c in range(CHUNKS):
             interleave(nc.scalar.copy, xb2[c][:, :, 0:2], g_low[:, :, c * CH : (c + 1) * CH])
-        gather(g_rows[:, 0:CHUNKS, :].rearrange("p c n -> p (c n)"), last, 2, 0, S)
-        for c in range(2):
-            nc.tensor.matmul_mx(
-                out=acc[c, 1][0:32].rearrange("p m j -> p (m j)"),
-                lhsT=w_sb[0, 0][:, 0:32].bitcast(FP8X4),
-                lhsT_scale=w_planes[:, 0:32],
-                rhs=words0[:].bitcast(FP8X4),
-                rhs_scale=plane0[:],
-                start=True,
-                stop=True,
-            )
+        gather(g_rows[:, 0:CHUNKS, :].rearrange("p c n -> p (c n)"), LAST, 2, 0, S)
 
         out_v = out.rearrange("(m p) j -> p m j", p=P)
         res = [keep.tile([P, MT, CH], F32, name="res%d" % c, align_bytes=256) for c in range(CHUNKS)]
 
-        def held(c, bank):
-            return slice(2 * bank, 2 * bank + 2) if c == 0 else slice(bank, MT, 2)
-
         def gather_last(c):
-            gather(g_high[c][:, 1, :], last, 3, c * CH, (c + 1) * CH)
+            gather(g_high[c][:, 1, :], LAST, 3, c * CH, (c + 1) * CH)
 
         def round_last(copy, c):
             interleave(copy, xb2[c][:, :, 2:4], g_high[c])
 
         def quantize_last(c):
-            quantize(last, c, c + 1, xb2[c], "codes_last%d" % c)
+            quantize(LAST, c, c + 1, xb2[c], "codes_last%d" % c)
 
         def leave(copy, c, bank):
-            tiles = held(c, bank)
+            tiles = slice(2 * bank, 2 * bank + 2)
             copy(res[c][:, tiles, :], acc[c, bank][:, 0:2, :])
             nc.sync.dma_start(out_v[:, tiles, c * CH : (c + 1) * CH], res[c][:, tiles, :])
 
@@ -191,18 +171,11 @@ def tile_list_heads_none_kernel(tc, xT, w_words, w_scales, wgt, offs, out):
         for c in (2, 3):
             quantize_last(c)
 
-        for pair in ((0, 1), (2, 3)):
-            for c in range(CHUNKS):
-                multiply(0, c, pair)
-        for c in range(CHUNKS):
-            multiply(1, c, (0, 1) if c < 2 else (0,))
-        multiply(last, 0, (0, 1))
-        leave(nc.scalar.copy, 0, 0)
-        for a in (1, last):
-            multiply(a, 0, (2, 3))
-        leave(nc.scalar.copy, 0, 1)
-        for c in range(1, CHUNKS):
+        for a in range(LAST):
             for bank in range(2):
-                multiply(1, c, (3, 1) if c >= 2 and bank == 1 else (2 + bank,))
-                multiply(last, c, (bank, 2 + bank))
-                leave(nc.scalar.copy if bank == 0 else nc.vector.tensor_copy, c, bank)
+                for c in range(CHUNKS):
+                    multiply(a, c, bank)
+        for c in range(CHUNKS):
+            for bank in range(2):
+                multiply(LAST, c, bank)
+                leave(nc.scalar.copy if bank == 0 or c == 0 else nc.vector.tensor_copy, c, bank)

@@ -53,11 +53,12 @@ def tile_list_heads_none_kernel(tc, xT, w_words, w_scales, wgt, offs, out):
         w_view = w_words.rearrange("a p n t -> p a (n t)").bitcast(I32)
         w_sb = {}
 
-        def load_weights(a, m0, m1):
-            words = keep.tile([P, (m1 - m0) * P], I32, name="w%d%d" % (a, m0), align_bytes=256)
-            nc.sync.dma_start(words[:], w_view[:, a, m0 * P : m1 * P])
-            for m in range(m0, m1):
-                w_sb[a, m] = words[:, (m - m0) * P : (m - m0 + 1) * P]
+        def load_weights(a0, a1, m0, m1):
+            words = keep.tile([P, a1 - a0, (m1 - m0) * P], I32, name="w%d%d" % (a0, m0), align_bytes=256)
+            nc.sync.dma_start(words[:], w_view[:, a0:a1, m0 * P : m1 * P])
+            for a in range(a0, a1):
+                for m in range(m0, m1):
+                    w_sb[a, m] = words[:, a - a0, (m - m0) * P : (m - m0 + 1) * P]
 
         x_sb = {}
         for a in range(PASSES):
@@ -66,15 +67,13 @@ def tile_list_heads_none_kernel(tc, xT, w_words, w_scales, wgt, offs, out):
                 paired = a == 0
                 width = 2 * T if paired and t % 2 == 0 else T
                 x_sb[a, t] = keep.tile([P, width], F32, name="x%d%d" % (a, t), tag="x%d%d" % (a, t), align_bytes=256)
-                if (a, t) == (LAST, 3):
-                    load_weights(0, 0, MT)
                 if not (paired and t % 2 == 1):
                     nc.sync.dma_start(x_sb[a, t][:], rows[:, t * T : t * T + width])
                 if (a, t) == (0, 0):
                     nc.sync.dma_start(offsets[:], offs)
-        load_weights(1, 0, 2)
-        load_weights(1, 2, MT)
-        load_weights(LAST, 0, MT)
+        for m0 in (0, 2):
+            load_weights(0, 1, m0, m0 + 2)
+            load_weights(1, PASSES, m0, m0 + 2)
 
         g = [keep.tile([P, 4, S], F32, name="g%d" % a) for a in range(LAST)]
         g_low = keep.tile([P, 2, S], F32, name="g_low")
@@ -97,23 +96,25 @@ def tile_list_heads_none_kernel(tc, xT, w_words, w_scales, wgt, offs, out):
         def interleave(copy, dst, src):
             copy(dst, src.rearrange("p t n -> p n t"))
 
-        def quantize(a, c0, c1, values, tag):
+        def codes(a, c0, c1, tag):
             width = (c1 - c0) * CH
             words = keep.tile([P, width], U32, name="codes%d%d" % (a, c0), tag=tag, align_bytes=256)
             plane = keep.tile([P, width], U8, name="scales%d%d" % (a, c0), align_bytes=64)
-            nc.vector.quantize_mx(
-                out=words[:].bitcast(FP8X4),
-                scales=plane[:],
-                in_=values[:].rearrange("p n t -> p (n t)"),
-            )
             for c in range(c0, c1):
                 cols = slice((c - c0) * CH, (c - c0 + 1) * CH)
                 operand[a, c] = (words[:, cols], plane[:, cols])
+            return words, plane
 
-        def multiply(a, c, bank):
+        def quantize(words, plane, values):
+            nc.vector.quantize_mx(out=words.bitcast(FP8X4), scales=plane, in_=values.rearrange("p n t -> p (n t)"))
+
+        def place(c, m):
+            return (m // 2, m % 2) if c == 0 else (m % 2, m // 2)
+
+        def multiply(a, c, tiles):
             words, plane = operand[a, c]
-            for slot in range(2):
-                m = 2 * bank + slot
+            for m in tiles:
+                bank, slot = place(c, m)
                 nc.tensor.matmul_mx(
                     out=acc[c, bank][:, slot, :],
                     lhsT=w_sb[a, m].bitcast(FP8X4),
@@ -135,11 +136,24 @@ def tile_list_heads_none_kernel(tc, xT, w_words, w_scales, wgt, offs, out):
                 else:
                     gather(g[a][:, t, :], a, t, 0, S)
                 if (a, t) == (1, 1):
-                    quantize(0, 0, CHUNKS, xb[0], "x11")
+                    words0, plane0 = codes(0, 0, CHUNKS, "x11")
+                    quantize(words0[:], plane0[:], xb[0][:])
             interleave(nc.scalar.copy, xb[a][:], g[a][:])
         for t in range(2):
             gather(g_low[:, t, :], LAST, t, 0, S)
-        quantize(1, 0, CHUNKS, xb[1], "x21")
+        words1, plane1 = codes(1, 0, CHUNKS, "x21")
+        quantize(words1[:, :CH], plane1[:, :CH], xb[1][:, :CH, :])
+        quantize(words1[:, CH:], plane1[:, CH:], xb[1][:, CH:, :])
+        for c in range(CHUNKS):
+            nc.tensor.matmul_mx(
+                out=acc[c, 1][0:32].rearrange("p m j -> p (m j)"),
+                lhsT=words1[:, 0:32].bitcast(FP8X4),
+                lhsT_scale=plane1[:, 0:32],
+                rhs=words0[:].bitcast(FP8X4),
+                rhs_scale=plane0[:],
+                start=True,
+                stop=True,
+            )
         for c in range(CHUNKS):
             interleave(nc.scalar.copy, xb2[c][:, :, 0:2], g_low[:, :, c * CH : (c + 1) * CH])
         gather(g_rows[:, 0:CHUNKS, :].rearrange("p c n -> p (c n)"), LAST, 2, 0, S)
@@ -154,10 +168,11 @@ def tile_list_heads_none_kernel(tc, xT, w_words, w_scales, wgt, offs, out):
             interleave(copy, xb2[c][:, :, 2:4], g_high[c])
 
         def quantize_last(c):
-            quantize(LAST, c, c + 1, xb2[c], "codes_last%d" % c)
+            words, plane = codes(LAST, c, c + 1, "codes_last%d" % c)
+            quantize(words[:], plane[:], xb2[c][:])
 
         def leave(copy, c, bank):
-            tiles = slice(2 * bank, 2 * bank + 2)
+            tiles = slice(2 * bank, 2 * bank + 2) if c == 0 else slice(bank, MT, 2)
             copy(res[c][:, tiles, :], acc[c, bank][:, 0:2, :])
             nc.sync.dma_start(out_v[:, tiles, c * CH : (c + 1) * CH], res[c][:, tiles, :])
 
@@ -172,10 +187,17 @@ def tile_list_heads_none_kernel(tc, xT, w_words, w_scales, wgt, offs, out):
             quantize_last(c)
 
         for a in range(LAST):
+            for c in range(CHUNKS):
+                multiply(a, c, (0, 1))
+        multiply(0, 0, (2, 3))
+        multiply(LAST, 0, (0, 1))
+        leave(nc.scalar.copy, 0, 0)
+        for a in (1, LAST):
+            multiply(a, 0, (2, 3))
+        leave(nc.scalar.copy, 0, 1)
+        for c in range(1, CHUNKS):
             for bank in range(2):
-                for c in range(CHUNKS):
-                    multiply(a, c, bank)
-        for c in range(CHUNKS):
-            for bank in range(2):
-                multiply(LAST, c, bank)
-                leave(nc.scalar.copy if bank == 0 or c == 0 else nc.vector.tensor_copy, c, bank)
+                for a in range(LAST):
+                    multiply(a, c, (2 + bank,))
+                multiply(LAST, c, (bank, 2 + bank))
+                leave(nc.vector.tensor_copy if c >= 2 and bank == 0 else nc.scalar.copy, c, bank)

@@ -67,13 +67,16 @@ def tile_list_heads_none_kernel(tc, xT, w_words, w_scales, wgt, offs, out):
                 paired = a == 0
                 width = 2 * T if paired and t % 2 == 0 else T
                 x_sb[a, t] = keep.tile([P, width], F32, name="x%d%d" % (a, t), tag="x%d%d" % (a, t), align_bytes=256)
+                if (a, t) == (LAST, 3):
+                    load_weights(0, 1, 0, 1)
                 if not (paired and t % 2 == 1):
                     nc.sync.dma_start(x_sb[a, t][:], rows[:, t * T : t * T + width])
                 if (a, t) == (0, 0):
                     nc.sync.dma_start(offsets[:], offs)
-        for m0 in (0, 2):
-            load_weights(0, 1, m0, m0 + 2)
-            load_weights(1, PASSES, m0, m0 + 2)
+        load_weights(0, 1, 1, 2)
+        load_weights(0, 1, 2, MT)
+        load_weights(1, PASSES, 0, 2)
+        load_weights(1, PASSES, 2, MT)
 
         g = [keep.tile([P, 4, S], F32, name="g%d" % a) for a in range(LAST)]
         g_low = keep.tile([P, 2, S], F32, name="g_low")
@@ -144,7 +147,7 @@ def tile_list_heads_none_kernel(tc, xT, w_words, w_scales, wgt, offs, out):
         words1, plane1 = codes(1, 0, CHUNKS, "x21")
         quantize(words1[:, :CH], plane1[:, :CH], xb[1][:, :CH, :])
         quantize(words1[:, CH:], plane1[:, CH:], xb[1][:, CH:, :])
-        for c in range(CHUNKS):
+        for c in range(3):
             nc.tensor.matmul_mx(
                 out=acc[c, 1][0:32].rearrange("p m j -> p (m j)"),
                 lhsT=words1[:, 0:32].bitcast(FP8X4),
@@ -174,7 +177,10 @@ def tile_list_heads_none_kernel(tc, xT, w_words, w_scales, wgt, offs, out):
         def leave(copy, c, bank):
             tiles = slice(2 * bank, 2 * bank + 2) if c == 0 else slice(bank, MT, 2)
             copy(res[c][:, tiles, :], acc[c, bank][:, 0:2, :])
-            nc.sync.dma_start(out_v[:, tiles, c * CH : (c + 1) * CH], res[c][:, tiles, :])
+            if c == 2:
+                tiles = slice(0, MT)
+            if c != 2 or bank == 1:
+                nc.sync.dma_start(out_v[:, tiles, c * CH : (c + 1) * CH], res[c][:, tiles, :])
 
         for c in range(3):
             gather_last(c)
@@ -186,10 +192,11 @@ def tile_list_heads_none_kernel(tc, xT, w_words, w_scales, wgt, offs, out):
         for c in (2, 3):
             quantize_last(c)
 
-        for a in range(LAST):
+        for tiles in ((0,), (1,), (2, 3)):
             for c in range(CHUNKS):
-                multiply(a, c, (0, 1))
-        multiply(0, 0, (2, 3))
+                multiply(0, c, tiles)
+        for c in range(CHUNKS):
+            multiply(1, c, (0, 1) if c < 2 else (0,))
         multiply(LAST, 0, (0, 1))
         leave(nc.scalar.copy, 0, 0)
         for a in (1, LAST):
@@ -197,7 +204,6 @@ def tile_list_heads_none_kernel(tc, xT, w_words, w_scales, wgt, offs, out):
         leave(nc.scalar.copy, 0, 1)
         for c in range(1, CHUNKS):
             for bank in range(2):
-                for a in range(LAST):
-                    multiply(a, c, (2 + bank,))
+                multiply(1, c, (3, 1) if c >= 2 and bank == 1 else (2 + bank,))
                 multiply(LAST, c, (bank, 2 + bank))
                 leave(nc.vector.tensor_copy if c >= 2 and bank == 0 else nc.scalar.copy, c, bank)

from contextlib import ExitStack

import concourse.mybir as mybir

K, M, T, S = 1536, 512, 2048, 512
FLOPS = 2 * K * M * S

F32 = mybir.dt.float32
BF16 = mybir.dt.bfloat16
I32 = mybir.dt.int32
U8 = mybir.dt.uint8
U16 = mybir.dt.uint16
U32 = mybir.dt.uint32
FP8X4 = mybir.dt.float8_e4m3fn_x4
MULT = mybir.AluOpType.mult

P = 128
PASSES = K // (4 * P)
LAST = PASSES - 1
CH = 128
CHUNKS = S // CH
MT = M // P
HALF = S // 2


def tile_list_heads_none_kernel(tc, xT, w_words, w_scales, wgt, offs, out):
    nc = tc.nc
    with ExitStack() as ctx:
        keep = ctx.enter_context(tc.tile_pool(name="keep", bufs=1))
        psum = ctx.enter_context(tc.psum_pool(name="psum", bufs=1))

        offsets = keep.tile([P, S // 16], U16, name="offsets")
        wgt_sb = keep.tile([P, S], F32, name="wgt_sb", align_bytes=64)
        wgt_rows = keep.tile([P, 32], F32, name="wgt_rows", align_bytes=64)
        wgt_cols = keep.tile([P, 32], F32, name="wgt_cols", align_bytes=64)
        wgt_spread = keep.tile([P, S], F32, name="wgt_spread", align_bytes=64)
        nc.scalar.dma_start(wgt_rows[:], wgt.rearrange("(g r) (b q) -> g r b q", r=16, q=32)[:, 0, :, :])
        nc.vector.transpose(wgt_cols[:], wgt_rows[:])
        nc.vector.tensor_copy(
            wgt_spread[:].rearrange("p (b e r) -> p b e r", e=2, r=16),
            wgt_cols[:].rearrange("p (e b) -> p b e", e=2).unsqueeze(3).to_broadcast([P, S // 32, 2, 16]),
        )
        nc.vector.transpose(wgt_sb[:], wgt_spread[:])

        w_planes = keep.tile([P, M], U8, name="w_planes", align_bytes=64)
        nc.gpsimd.memset(w_planes[:].bitcast(I32), 0)
        for q in range(4):
            nc.gpsimd.dma_start(
                w_planes[32 * q : 32 * q + 4 * PASSES, :].bitcast(I32),
                w_scales[:, 4 * q : 4 * q + 4, :].bitcast(I32),
            )

        w_view = w_words.rearrange("a p n t -> p a (n t)").bitcast(I32)
        w_sb = {}

        def load_weights(a0, a1, m0, m1):
            words = keep.tile([P, a1 - a0, (m1 - m0) * P], I32, name="w%d%d" % (a0, m0), align_bytes=256)
            nc.sync.dma_start(words[:], w_view[:, a0:a1, m0 * P : m1 * P])
            for a in range(a0, a1):
                for m in range(m0, m1):
                    w_sb[a, m] = words[:, a - a0, (m - m0) * P : (m - m0 + 1) * P]

        x_sb = {}
        for a in range(PASSES):
            rows = xT[4 * P * a : 4 * P * (a + 1), :].rearrange("(p t) c -> p (t c)", t=4)
            for t in range(4):
                paired = a == 0
                width = 2 * T if paired and t % 2 == 0 else T
                x_sb[a, t] = keep.tile([P, width], F32, name="x%d%d" % (a, t), tag="x%d%d" % (a, t), align_bytes=256)
                if (a, t) == (LAST, 3):
                    load_weights(0, 1, 0, 1)
                if not (paired and t % 2 == 1):
                    nc.sync.dma_start(x_sb[a, t][:], rows[:, t * T : t * T + width])
                if (a, t) == (0, 0):
                    nc.sync.dma_start(offsets[:], offs)
        load_weights(0, 1, 1, 2)
        load_weights(0, 1, 2, MT)
        load_weights(1, PASSES, 0, 2)
        load_weights(1, PASSES, 2, MT)

        g = [keep.tile([P, 4, S], F32, name="g%d" % a) for a in range(LAST)]
        g_low = keep.tile([P, 2, S], F32, name="g_low")
        g_rows = keep.tile([P, CHUNKS + 3, CH], F32, name="g_rows")
        g_high = [g_rows[:, c : CHUNKS + c % 3 + 1 : CHUNKS + c % 3 - c, :] for c in range(CHUNKS)]
        acc = {}
        for c in range(CHUNKS):
            for b in range(2):
                acc[c, b] = psum.tile([P, 4, CH], F32, name="acc%d%d" % (c, b))
        operand = {}

        def gather(dst, a, t, j0, j1):
            nc.vector.tensor_tensor(
                dst,
                x_sb[a, t][:].indirect(offsets[:, j0 // 16 : j1 // 16]),
                wgt_sb[:, j0:j1],
                MULT,
            )

        def interleave(copy, dst, src):
            copy(dst, src.rearrange("p t n -> p n t"))

        def codes(a, c0, c1, tag):
            width = (c1 - c0) * CH
            words = keep.tile([P, width], U32, name="codes%d%d" % (a, c0), tag=tag, align_bytes=256)
            plane = keep.tile([P, width], U8, name="scales%d%d" % (a, c0), align_bytes=64)
            for c in range(c0, c1):
                cols = slice((c - c0) * CH, (c - c0 + 1) * CH)
                operand[a, c] = (words[:, cols], plane[:, cols])
            return words, plane

        def quantize(words, plane, values):
            nc.vector.quantize_mx(out=words.bitcast(FP8X4), scales=plane, in_=values.rearrange("p n t -> p (n t)"))

        def place(c, m):
            return (m // 2, m % 2) if c == 0 else (m % 2, m // 2)

        def multiply(a, c, tiles):
            words, plane = operand[a, c]
            for m in tiles:
                bank, slot = place(c, m)
                nc.tensor.matmul_mx(
                    out=acc[c, bank][:, slot, :],
                    lhsT=w_sb[a, m].bitcast(FP8X4),
                    lhsT_scale=w_planes[4 * a : P, m * P : (m + 1) * P],
                    rhs=words.bitcast(FP8X4),
                    rhs_scale=plane,
                    start=(a == 0 and slot == 0),
                    stop=(a == LAST and slot == 1),
                )

        xb = [keep.tile([P, S, 4], BF16, name="xb%d" % a, align_bytes=64) for a in range(LAST)]
        xb2 = [keep.tile([P, CH, 4], BF16, name="xb2%d" % c, align_bytes=64) for c in range(CHUNKS)]
        for a in range(LAST):
            for t in range(4):
                if a == 0 and t % 2 == 0:
                    nc.scalar.copy(x_sb[a, t + 1][:], x_sb[a, t][:, T:])
                    gather(g[a][:, t, :HALF], a, t, 0, HALF)
                    gather(g[a][:, t, HALF:], a, t, HALF, S)
                else:
                    gather(g[a][:, t, :], a, t, 0, S)
                if (a, t) == (1, 1):
                    words0, plane0 = codes(0, 0, CHUNKS, "x11")
                    quantize(words0[:], plane0[:], xb[0][:])
            interleave(nc.scalar.copy, xb[a][:], g[a][:])
        for t in range(2):
            gather(g_low[:, t, :], LAST, t, 0, S)
        words1, plane1 = codes(1, 0, CHUNKS, "x21")
        quantize(words1[:, :CH], plane1[:, :CH], xb[1][:, :CH, :])
        quantize(words1[:, CH:], plane1[:, CH:], xb[1][:, CH:, :])
        for c in range(3):
            nc.tensor.matmul_mx(
                out=acc[c, 1][0:32].rearrange("p m j -> p (m j)"),
                lhsT=words1[:, 0:32].bitcast(FP8X4),
                lhsT_scale=plane1[:, 0:32],
                rhs=words0[:].bitcast(FP8X4),
                rhs_scale=plane0[:],
                start=True,
                stop=True,
            )
        for c in range(CHUNKS):
            interleave(nc.scalar.copy, xb2[c][:, :, 0:2], g_low[:, :, c * CH : (c + 1) * CH])
        gather(g_rows[:, 0:CHUNKS, :].rearrange("p c n -> p (c n)"), LAST, 2, 0, S)

        out_v = out.rearrange("(m p) j -> p m j", p=P)
        res = [keep.tile([P, MT, CH], F32, name="res%d" % c, align_bytes=256) for c in range(CHUNKS)]

        def gather_last(c):
            gather(g_high[c][:, 1, :], LAST, 3, c * CH, (c + 1) * CH)

        def round_last(copy, c):
            interleave(copy, xb2[c][:, :, 2:4], g_high[c])

        def quantize_last(c):
            words, plane = codes(LAST, c, c + 1, "codes_last%d" % c)
            quantize(words[:], plane[:], xb2[c][:])

        def leave(copy, c, bank):
            tiles = slice(2 * bank, 2 * bank + 2) if c == 0 else slice(bank, MT, 2)
            copy(res[c][:, tiles, :], acc[c, bank][:, 0:2, :])
            if c == 2:
                tiles = slice(0, MT)
            if c != 2 or bank == 1:
                nc.sync.dma_start(out_v[:, tiles, c * CH : (c + 1) * CH], res[c][:, tiles, :])

        for c in range(3):
            gather_last(c)
            round_last(nc.scalar.copy, c)
        quantize_last(0)
        gather_last(3)
        quantize_last(1)
        round_last(nc.vector.tensor_copy, 3)
        for c in (2, 3):
            quantize_last(c)

        for tiles in ((0,), (1,), (2, 3)):
            for c in range(CHUNKS):
                multiply(0, c, tiles)
        for c in range(CHUNKS):
            multiply(1, c, (0, 1) if c < 2 else (0,))
        multiply(LAST, 0, (0, 1))
        leave(nc.scalar.copy, 0, 0)
        for a in (1, LAST):
            multiply(a, 0, (2, 3))
        leave(nc.scalar.copy, 0, 1)
        for c in range(1, CHUNKS):
            for bank in range(2):
                multiply(1, c, (3, 1) if c >= 2 and bank == 1 else (2 + bank,))
                multiply(LAST, c, (bank, 2 + bank))
                leave(nc.vector.tensor_copy if c >= 2 and bank == 0 else nc.scalar.copy, c, bank)
